import numpy as np
import ml_dtypes


def mxq(x, axis, fmt="e4m3"):
    dtype, down = {"e4m3": (ml_dtypes.float8_e4m3fn, 7), "e5m2": (ml_dtypes.float8_e5m2, 14)}[fmt]
    v = np.moveaxis(np.asarray(x, np.float32).astype(ml_dtypes.bfloat16).astype(np.float64), axis, -1)
    blocks = v.reshape(v.shape[:-1] + (-1, 32))
    amax = np.abs(blocks).max(-1, keepdims=True)
    byte = np.maximum(np.where(amax > 0, np.frexp(amax)[1] - 1 + 127, 0) - down, 1)
    scale = np.exp2(byte - 127.0)
    codes = (blocks / scale).astype(np.float32).astype(dtype).astype(np.float64)
    return np.moveaxis((codes * scale).reshape(v.shape), -1, axis)


WIDE = False


def mx_kscale(k):
    if not WIDE:
        return np.ones(k)
    levels = np.array([10, -10, 5, -5, 0])
    if k % 512:
        return np.exp2(np.random.permutation(np.resize(levels, k // 32))).repeat(32)
    a = np.empty((k // 512, 16))
    for p in range(k // 512):
        a[p, :8] = np.random.permutation(np.resize(levels, 8))
        for g in range(8):
            far = levels[np.abs(levels - a[p, g]) >= 10]
            a[p, g + 8] = far[np.random.randint(len(far))]
    return np.exp2(a.ravel()).repeat(32)


def f64(x):
    return np.asarray(x).astype(np.float64)


def striped(idx):
    return np.tile(idx.reshape(-1, 16).T, (8, 1)).astype(np.uint16)


def unstriped(offs):
    return offs[:16].T.reshape(-1).astype(np.int64)


E2M1 = np.array([0.0, 0.5, 1.0, 1.5, 2.0, 3.0, 4.0, 6.0, -0.0, -0.5, -1.0, -1.5, -2.0, -3.0, -4.0, -6.0])


def pack_weight(w, fmt):
    k, n = w.shape
    w = f64(np.asarray(w, np.float32).astype(ml_dtypes.bfloat16)).reshape(k // 32, 32, n)
    amax = np.abs(w).max(1)
    if fmt == "e4m3":
        byte = np.frexp(amax)[1] - 1 + 127 - 7
    else:
        mant, ex = np.frexp(amax / 6.0)
        byte = np.where(mant > 0.5, ex, ex - 1) + 127
    byte = np.clip(np.where(amax > 0, byte, 1), 1, 254)
    scaled = (w * np.exp2(127.0 - byte)[:, None, :]).reshape(k, n).astype(np.float32)
    by_word = np.ascontiguousarray(scaled.reshape(k // 512, 128, 4, n).transpose(0, 1, 3, 2))
    if fmt == "e4m3":
        words = by_word.astype(ml_dtypes.float8_e4m3fn).view(np.uint8)
    else:
        c = by_word.astype(ml_dtypes.float4_e2m1fn).view(np.uint8) & 0xF
        words = (c[..., 0::2] | (c[..., 1::2] << 4)).reshape(k // 512, 128, 2 * n)
    return np.ascontiguousarray(words), np.ascontiguousarray(byte.astype(np.uint8).reshape(k // 512, 16, n))


def unpack_weight(words, scales, fmt):
    g, _, n = scales.shape
    words = np.ascontiguousarray(words).reshape(g, 128, n, -1)
    if fmt == "e4m3":
        vals = words.view(ml_dtypes.float8_e4m3fn).astype(np.float64)
    else:
        nib = np.empty((g, 128, n, 4), np.uint8)
        nib[..., 0::2] = words & 0xF
        nib[..., 1::2] = words >> 4
        vals = E2M1[nib]
    vals = vals * np.repeat(np.exp2(scales.astype(np.float64) - 127.0), 8, axis=1)[..., None]
    return vals.transpose(0, 1, 3, 2).reshape(g * 512, n)


def gelu(v):
    return 0.5 * v * (1.0 + np.tanh(np.sqrt(2.0 / np.pi) * (v + 0.044715 * v**3)))


T, S, P, P2, K, H, N = 4096, 2048, 1024, 512, 1024, 512, 768


def setup_inputs():
    n = np.random.standard_normal
    s = mx_kscale(K)[:, None]
    u = mx_kscale(H)[:, None]
    tab_words, tab_scales = pack_weight(n((K, T)) * s, "e4m3")
    w4_words, w4_scales = pack_weight(1.3 * n((H, N)) / np.sqrt(H) / (u * u), "e2m1")
    return {
        "tab_words": tab_words,
        "tab_scales": tab_scales,
        "offs": striped(np.random.permutation(T)[:S]),
        "pos1": striped(np.random.permutation(S)[:P]),
        "pos2": striped(np.random.permutation(S)[:P]),
        "pos3": striped(np.random.permutation(P)[:P2]),
        "pos4": striped(np.random.permutation(S)[:P2]),
        "w1": (1.2 * n((K, H)) / np.sqrt(K) / s).astype(np.float32),
        "gain": (np.random.uniform(0.6, 1.6, H) * u[:, 0]).astype(np.float32),
        "ws": (0.53 * n((H, N)) / np.sqrt(H) / (u * u)).astype(np.float32),
        "w4_words": w4_words,
        "w4_scales": w4_scales,
    }


def reference(tab_words, tab_scales, offs, pos1, pos2, pos3, pos4, w1, gain, ws, w4_words, w4_scales):
    v = unpack_weight(tab_words, tab_scales, "e4m3")[:, unstriped(offs)]
    w1q = mxq(f64(w1), 0, "e4m3")
    h = f64(gain)[:, None] * np.tanh(w1q.T @ v)
    a1 = h[:, unstriped(pos1)] + h[:, unstriped(pos2)]
    a2 = a1[:, unstriped(pos3)] * h[:, unstriped(pos4)]
    a2q = mxq(a2, 0, "e4m3")
    wsq = mxq(f64(ws), 0, "e4m3")
    w4 = unpack_weight(w4_words, w4_scales, "e2m1")
    phase = wsq.T @ a2q
    lean = w4.T @ a2q
    return np.sin(phase) * np.tanh(lean)

@@ -1,0 +1,264 @@
+import math
+from contextlib import ExitStack
+
+import concourse.mybir as mybir
+
+T, S, PJ, PK, K, H, N = 4096, 2048, 1024, 512, 1024, 512, 768
+FLOPS = 2 * K * H * S + 2 * 2 * H * N * PK
+
+F32 = mybir.dt.float32
+BF16 = mybir.dt.bfloat16
+I32 = mybir.dt.int32
+U32 = mybir.dt.uint32
+U16 = mybir.dt.uint16
+U8 = mybir.dt.uint8
+FP8X4 = mybir.dt.float8_e4m3fn_x4
+FP4X4 = mybir.dt.float4_e2m1fn_x4
+ALU = mybir.AluOpType
+ACT = mybir.ActivationFunctionType
+
+P = 128
+PACK = 4
+K_PASS = P * PACK
+PASSES = K // K_PASS
+BANK = 512
+LANES = 16
+J_TILE = 128
+HALF = 3
+TURN = 2.0 * math.pi
+ROUNDER = 1.5 * 2.0**23
+
+
+def tile_list_scrap_join_fit_kernel(
+    tc, tab_words, tab_scales, offs, pos1, pos2, pos3, pos4, w1, gain, ws, w4_words, w4_scales, out
+):
+    nc = tc.nc
+    with ExitStack() as ctx:
+        keep = ctx.enter_context(tc.tile_pool(name="keep", bufs=1))
+        ring = ctx.enter_context(tc.tile_pool(name="ring", bufs=2))
+        deep = ctx.enter_context(tc.tile_pool(name="deep", bufs=4))
+        six = ctx.enter_context(tc.tile_pool(name="six", bufs=6))
+        psum = ctx.enter_context(tc.psum_pool(name="psum", bufs=8))
+
+        offs_sb = keep.tile([P, S // LANES], U16)
+        pos1_sb = keep.tile([P, PJ // LANES], U16)
+        pos2_sb = keep.tile([P, PJ // LANES], U16)
+        pos3_sb = keep.tile([P, PK // LANES], U16)
+        pos4_sb = keep.tile([P, PK // LANES], U16)
+        tab_sc = keep.tile([P, T], U8, align_bytes=64)
+        w4_sc = keep.tile([P, N], U8, align_bytes=64)
+        nc.vector.memset(tab_sc[:].bitcast(I32), 0)
+        nc.vector.memset(w4_sc[:].bitcast(I32), 0)
+        nc.sync.dma_start(offs_sb[:], offs)
+        tab_w = [keep.tile([P, T], U32, align_bytes=64, name=f"tab_w{a}") for a in range(PASSES)]
+        w1_pieces = [(0, 0, 256), (0, 256, 256), (1, 0, 256), (1, 256, 128), (1, 384, 128)]
+        w1_raw = [keep.tile([P, PACK, n], F32, name=f"w1_raw{i}") for i, (a, c0, n) in enumerate(w1_pieces)]
+
+        def load_words(a):
+            nc.sync.dma_start(tab_w[a][:].bitcast(I32), tab_words[a].rearrange("p t i -> p (t i)").bitcast(I32))
+
+        def load_w1(i):
+            a, c0, n = w1_pieces[i]
+            rows = w1[a * K_PASS : (a + 1) * K_PASS, :].rearrange("(p j) c -> p j c", j=PACK)
+            nc.sync.dma_start(w1_raw[i][:], rows[:, :, c0 : c0 + n])
+
+        load_w1(0)
+        for q in range(4):
+            nc.sync.dma_start(
+                tab_sc[32 * q : 32 * q + 4 * PASSES, :].bitcast(I32),
+                tab_scales[:, 4 * q : 4 * q + 4, :].bitcast(I32),
+            )
+        load_words(0)
+        load_w1(1)
+        load_words(1)
+        for i in range(2, len(w1_pieces)):
+            load_w1(i)
+        gain_sb = keep.tile([P, PACK], F32)
+        nc.sync.dma_start(gain_sb[:], gain.rearrange("(p t) -> p t", t=PACK))
+        nc.sync.dma_start(pos1_sb[:], pos1)
+        nc.sync.dma_start(pos2_sb[:], pos2)
+        nc.sync.dma_start(pos4_sb[:], pos4)
+        nc.sync.dma_start(pos3_sb[:], pos3)
+        ws_raw = keep.tile([P, PACK, N], F32)
+        nc.sync.dma_start(ws_raw[:], ws.rearrange("(p j) n -> p j n", j=PACK))
+        w4_w = keep.tile([P, 2 * N], U8, align_bytes=64)
+        nc.sync.dma_start(w4_w[:].bitcast(I32), w4_words[0].bitcast(I32))
+        for q in range(4):
+            nc.sync.dma_start(
+                w4_sc[32 * q : 32 * q + 4, :].bitcast(I32), w4_scales[0, 4 * q : 4 * q + 4, :].bitcast(I32)
+            )
+
+        v_sc = keep.tile([P, S], U8, align_bytes=64)
+        nc.vector.tensor_copy(v_sc[:], tab_sc[:].indirect(offs_sb[:]))
+        v_w0 = keep.tile([P, S], U32, align_bytes=64)
+        nc.vector.tensor_copy(v_w0[:], tab_w[0][:].indirect(offs_sb[:]))
+
+        w1_bf0 = keep.tile([P, PACK, P, PACK], BF16, align_bytes=64)
+        w1_bf1 = keep.tile([P, PACK, P, PACK], BF16, align_bytes=64, tag="shared")
+        w1_bf = [w1_bf0, w1_bf1]
+        w1_w = [keep.tile([P, H], U32, align_bytes=64, name=f"w1_w{a}") for a in range(PASSES)]
+        w1_sc = [keep.tile([P, H], U8, align_bytes=64, name=f"w1_sc{a}") for a in range(PASSES)]
+
+        def weave_w1(i):
+            a, c0, n = w1_pieces[i]
+            nc.scalar.copy(
+                w1_bf[a][:, :, c0 // PACK : (c0 + n) // PACK, :].rearrange("p t m j -> p m j t"),
+                w1_raw[i][:].rearrange("p j (m t) -> p m j t", t=PACK),
+            )
+
+        def quantize_w1(a):
+            nc.vector.quantize_mx(
+                out=w1_w[a][:].bitcast(FP8X4), scales=w1_sc[a][:], in_=w1_bf[a][:].rearrange("p t m j -> p (t m j)")
+            )
+
+        v_w1 = []
+
+        def gather_words_1(c, tag):
+            picked = keep.tile([P, BANK], U32, align_bytes=64, name=f"v_w1_{c}", tag=tag)
+            nc.vector.tensor_copy(picked[:], tab_w[1][:].indirect(offs_sb[:, c * BANK // LANES : (c + 1) * BANK // LANES]))
+            v_w1.append(picked)
+
+        weave_w1(0)
+        weave_w1(1)
+        quantize_w1(0)
+        for i in range(2, len(w1_pieces)):
+            weave_w1(i)
+        for c in range(S // BANK - 1):
+            gather_words_1(c, f"v_w1_{c}")
+        quantize_w1(1)
+        gather_words_1(S // BANK - 1, "shared")
+
+        h = [keep.tile([P, S], F32, name=f"h{t}") for t in range(PACK)]
+        a1 = [keep.tile([P, PJ], F32, name=f"a1_{t}") for t in range(PACK)]
+        third = keep.tile([P, PACK, PK], F32)
+
+        def features(t):
+            for c in range(S // BANK):
+                cols = slice(c * BANK, (c + 1) * BANK)
+                acc = psum.tile([P, BANK], F32, name="bank")
+                for a in range(PASSES):
+                    nc.tensor.matmul_mx(
+                        out=acc[:],
+                        lhsT=w1_w[a][:, t * P : (t + 1) * P].bitcast(FP8X4),
+                        lhsT_scale=w1_sc[a][:, t * P : (t + 1) * P],
+                        rhs=(v_w0[:, cols] if a == 0 else v_w1[c][:]).bitcast(FP8X4),
+                        rhs_scale=v_sc[4 * a : P, cols],
+                        start=(a == 0),
+                        stop=(a == PASSES - 1),
+                    )
+                edge = deep.tile([P, BANK], F32)
+                nc.scalar.activation(edge[:], acc[:], ACT.Tanh)
+                if t == 0:
+                    nc.vector.tensor_scalar(h[t][:, cols], edge[:], gain_sb[:, t : t + 1], None, ALU.mult)
+                else:
+                    nc.scalar.activation(h[t][:, cols], edge[:], ACT.Copy, scale=gain_sb[:, t : t + 1])
+
+        for t in range(PACK):
+            features(t)
+            first = ring.tile([P, PJ], F32)
+            nc.vector.tensor_copy(first[:], h[t][:].indirect(pos1_sb[:]))
+            nc.vector.tensor_copy(third[:, t, :], h[t][:].indirect(pos4_sb[:]))
+            nc.vector.tensor_tensor(a1[t][:], h[t][:].indirect(pos2_sb[:]), first[:], ALU.add)
+
+        ws_bf = keep.tile([P, N, PACK], BF16, align_bytes=64)
+        ws_w = keep.tile([P, N], U32, align_bytes=64)
+        ws_sc = keep.tile([P, N], U8, align_bytes=64)
+        for u in range(2):
+            cols = slice(u * N // 2, (u + 1) * N // 2)
+            nc.scalar.copy(
+                ws_bf[:, cols, :].rearrange("p (c i) j -> p c j i", i=4),
+                ws_raw[:, :, cols].rearrange("p j (c i) -> p c j i", i=4),
+            )
+            nc.vector.quantize_mx(
+                out=ws_w[:, cols].bitcast(FP8X4), scales=ws_sc[:, cols], in_=ws_bf[:, cols, :].rearrange("p n j -> p (n j)")
+            )
+
+        out_v = out.rearrange("(b p) j -> p b j", p=P)
+
+        swap = [keep.tile([P, 2 * HALF * J_TILE], F32, name=f"swap{i}") for i in range(2)]
+
+        def products(c):
+            a2 = swap[c % 2][:, : PACK * J_TILE].rearrange("p (t j) -> p t j", t=PACK)
+            for t in range(PACK):
+                nc.vector.tensor_tensor(
+                    a2[:, t, :],
+                    a1[t][:].indirect(pos3_sb[:, c * J_TILE // LANES : (c + 1) * J_TILE // LANES]),
+                    third[:, t, c * J_TILE : (c + 1) * J_TILE],
+                    ALU.mult,
+                )
+            a2_bf = ring.tile([P, J_TILE, PACK], BF16, align_bytes=64)
+            nc.vector.tensor_copy(
+                a2_bf[:].rearrange("p (c i) t -> p c t i", i=4), a2.rearrange("p t (c i) -> p c t i", i=4)
+            )
+            a2_w = ring.tile([P, J_TILE], U32, align_bytes=64)
+            a2_sc = ring.tile([P, J_TILE], U8, align_bytes=64)
+            nc.vector.quantize_mx(
+                out=a2_w[:].bitcast(FP8X4), scales=a2_sc[:], in_=a2_bf[:].rearrange("p j t -> p (j t)")
+            )
+            parts = []
+            leans = []
+            for u in range(2):
+                phase = psum.tile([P, BANK], F32, name="bank")
+                lean = psum.tile([P, BANK], F32, name="bank")
+                for b in range(HALF):
+                    n0 = (u * HALF + b) * P
+                    nc.tensor.matmul_mx(
+                        out=phase[:, b * J_TILE : (b + 1) * J_TILE],
+                        lhsT=ws_w[:, n0 : n0 + P].bitcast(FP8X4),
+                        lhsT_scale=ws_sc[:, n0 : n0 + P],
+                        rhs=a2_w[:].bitcast(FP8X4),
+                        rhs_scale=a2_sc[:],
+                        start=True,
+                        stop=True,
+                    )
+                for b in range(HALF):
+                    n0 = (u * HALF + b) * P
+                    nc.tensor.matmul_mx(
+                        out=lean[:, b * J_TILE : (b + 1) * J_TILE],
+                        lhsT=w4_w[:, 2 * n0 : 2 * (n0 + P)].bitcast(FP4X4),
+                        lhsT_scale=w4_sc[:, n0 : n0 + P],
+                        rhs=a2_w[:].bitcast(FP8X4),
+                        rhs_scale=a2_sc[:],
+                        start=True,
+                        stop=True,
+                    )
+                width = HALF * J_TILE
+                turns = swap[c % 2][:, u * width : (u + 1) * width]
+                whole = deep.tile([P, width], U32)
+                slope = six.tile([P, width], F32)
+                nc.scalar.activation(turns, phase[:, :width], ACT.Copy, scale=1.0 / TURN)
+                nc.scalar.activation(whole[:], phase[:, :width], ACT.Copy, scale=1.0 / TURN, bias=ROUNDER)
+                parts.append((turns, whole, slope))
+                leans.append(lean)
+            for u in range(2):
+                nc.scalar.activation(parts[u][2][:], leans[u][:, : HALF * J_TILE], ACT.Tanh)
+            return parts
+
+        def reduce_phase(parts):
+            waves = []
+            for turns, whole, slope in parts:
+                rest = ring.tile([P, HALF * J_TILE], F32)
+                nc.vector.scalar_tensor_tensor(
+                    rest[:], whole[:].bitcast(I32), ROUNDER, turns, ALU.subtract, ALU.subtract
+                )
+                wave = deep.tile([P, HALF * J_TILE], F32)
+                nc.scalar.activation(wave[:], rest[:], ACT.Sin, scale=-TURN)
+                waves.append((wave, slope))
+            return waves
+
+        def finish(c, waves):
+            for u, (wave, slope) in enumerate(waves):
+                fit = deep.tile([P, HALF, J_TILE], F32)
+                nc.vector.tensor_tensor(fit[:].rearrange("p b j -> p (b j)"), wave[:], slope[:], ALU.mult)
+                nc.sync.dma_start(out_v[:, u * HALF : (u + 1) * HALF, c * J_TILE : (c + 1) * J_TILE], fit[:])
+
+        chunks = PK // J_TILE
+        parts = {}
+        waves = {}
+        for step in range(chunks + 2):
+            if step < chunks:
+                parts[step] = products(step)
+            if 2 <= step:
+                finish(step - 2, waves[step - 2])
+            if 1 <= step <= chunks:
+                waves[step - 1] = reduce_phase(parts[step - 1])

@@ -88,6 +88,10 @@ def tile_list_scrap_join_fit_kernel(
                 w4_sc[32 * q : 32 * q + 4, :].bitcast(I32), w4_scales[0, 4 * q : 4 * q + 4, :].bitcast(I32)
             )
 
+        seed = keep.tile([P, 1], F32)
+        preload = keep.tile([P, 1], F32)
+        nc.gpsimd.memset(seed[:], 0.0)
+        nc.scalar.activation(preload[:], seed[:], ACT.Silu)
         v_sc = keep.tile([P, S], U8, align_bytes=64)
         nc.vector.tensor_copy(v_sc[:], tab_sc[:].indirect(offs_sb[:]))
         v_w0 = keep.tile([P, S], U32, align_bytes=64)
@@ -130,7 +134,7 @@ def tile_list_scrap_join_fit_kernel(
 
         h = [keep.tile([P, S], F32, name=f"h{t}") for t in range(PACK)]
         a1 = [keep.tile([P, PJ], F32, name=f"a1_{t}") for t in range(PACK)]
-        third = keep.tile([P, PACK, PK], F32)
+        third = keep.tile([P, PACK, PK // 2], F32)
 
         def features(t):
             for c in range(S // BANK):
@@ -157,7 +161,7 @@ def tile_list_scrap_join_fit_kernel(
             features(t)
             first = ring.tile([P, PJ], F32)
             nc.vector.tensor_copy(first[:], h[t][:].indirect(pos1_sb[:]))
-            nc.vector.tensor_copy(third[:, t, :], h[t][:].indirect(pos4_sb[:]))
+            nc.vector.tensor_copy(third[:, t, :], h[t][:].indirect(pos4_sb[:, : PK // 2 // LANES]))
             nc.vector.tensor_tensor(a1[t][:], h[t][:].indirect(pos2_sb[:]), first[:], ALU.add)
 
         ws_bf = keep.tile([P, N, PACK], BF16, align_bytes=64)
@@ -177,17 +181,25 @@ def tile_list_scrap_join_fit_kernel(
 
         swap = [keep.tile([P, 2 * HALF * J_TILE], F32, name=f"swap{i}") for i in range(2)]
 
+        late = []
+
+        def third_of(t, c):
+            if c < 2:
+                return third[:, t, c * J_TILE : (c + 1) * J_TILE]
+            return late[t // 2][:, t % 2, (c - 2) * J_TILE : (c - 1) * J_TILE]
+
         def products(c):
             a2 = swap[c % 2][:, : PACK * J_TILE].rearrange("p (t j) -> p t j", t=PACK)
             for t in range(PACK):
                 nc.vector.tensor_tensor(
                     a2[:, t, :],
                     a1[t][:].indirect(pos3_sb[:, c * J_TILE // LANES : (c + 1) * J_TILE // LANES]),
-                    third[:, t, c * J_TILE : (c + 1) * J_TILE],
+                    third_of(t, c),
                     ALU.mult,
                 )
-            a2_bf = ring.tile([P, J_TILE, PACK], BF16, align_bytes=64)
-            nc.vector.tensor_copy(
+            a2_bf = keep.tile([P, J_TILE, PACK], BF16, align_bytes=64, name=f"a2_bf{c}", tag=f"late{c}")
+            weave = nc.scalar.copy if c < 2 else nc.vector.tensor_copy
+            weave(
                 a2_bf[:].rearrange("p (c i) t -> p c t i", i=4), a2.rearrange("p t (c i) -> p c t i", i=4)
             )
             a2_w = ring.tile([P, J_TILE], U32, align_bytes=64)
@@ -195,6 +207,14 @@ def tile_list_scrap_join_fit_kernel(
             nc.vector.quantize_mx(
                 out=a2_w[:].bitcast(FP8X4), scales=a2_sc[:], in_=a2_bf[:].rearrange("p j t -> p (j t)")
             )
+            if c < 2:
+                pair = keep.tile([P, 2, PK // 2], F32, align_bytes=64, name=f"late_third{c}", tag=f"late{c}")
+                for i in range(2):
+                    nc.vector.tensor_copy(pair[:, i, :], h[2 * c + i][:].indirect(pos4_sb[:, PK // 2 // LANES :]))
+                late.append(pair)
+            return a2_w, a2_sc
+
+        def multiply(c, a2_w, a2_sc):
             parts = []
             leans = []
             for u in range(2):
@@ -227,7 +247,12 @@ def tile_list_scrap_join_fit_kernel(
                 whole = deep.tile([P, width], U32)
                 slope = six.tile([P, width], F32)
                 nc.scalar.activation(turns, phase[:, :width], ACT.Copy, scale=1.0 / TURN)
-                nc.scalar.activation(whole[:], phase[:, :width], ACT.Copy, scale=1.0 / TURN, bias=ROUNDER)
+                if c == PK // J_TILE - 1:
+                    nc.vector.tensor_scalar(
+                        whole[:].bitcast(I32), phase[:, :width], 1.0 / TURN, ROUNDER, ALU.mult, ALU.add
+                    )
+                else:
+                    nc.scalar.activation(whole[:], phase[:, :width], ACT.Copy, scale=1.0 / TURN, bias=ROUNDER)
                 parts.append((turns, whole, slope))
                 leans.append(lean)
             for u in range(2):
@@ -255,9 +280,12 @@ def tile_list_scrap_join_fit_kernel(
         chunks = PK // J_TILE
         parts = {}
         waves = {}
+        codes = {0: products(0), 1: products(1)}
         for step in range(chunks + 2):
+            if 2 <= step < chunks:
+                codes[step] = products(step)
             if step < chunks:
-                parts[step] = products(step)
+                parts[step] = multiply(step, *codes[step])
             if 2 <= step:
                 finish(step - 2, waves[step - 2])
             if 1 <= step <= chunks:

@@ -98,21 +98,23 @@ def tile_list_scrap_join_fit_kernel(
         nc.vector.tensor_copy(v_w0[:], tab_w[0][:].indirect(offs_sb[:]))
 
         w1_bf0 = keep.tile([P, PACK, P, PACK], BF16, align_bytes=64)
-        w1_bf1 = keep.tile([P, PACK, P, PACK], BF16, align_bytes=64, tag="shared")
-        w1_bf = [w1_bf0, w1_bf1]
+        w1_lead = keep.tile([P, 1, P, PACK], BF16, align_bytes=64, tag="shared")
+        w1_rest = keep.tile([P, PACK - 1, P, PACK], BF16, align_bytes=64)
         w1_w = [keep.tile([P, H], U32, align_bytes=64, name=f"w1_w{a}") for a in range(PASSES)]
         w1_sc = [keep.tile([P, H], U8, align_bytes=64, name=f"w1_sc{a}") for a in range(PASSES)]
 
-        def weave_w1(i):
+        def weave_w1(i, woven, t0, t1):
             a, c0, n = w1_pieces[i]
             nc.scalar.copy(
-                w1_bf[a][:, :, c0 // PACK : (c0 + n) // PACK, :].rearrange("p t m j -> p m j t"),
-                w1_raw[i][:].rearrange("p j (m t) -> p m j t", t=PACK),
+                woven[:, :, c0 // PACK : (c0 + n) // PACK, :].rearrange("p t m j -> p m j t"),
+                w1_raw[i][:].rearrange("p j (m t) -> p m j t", t=PACK)[:, :, :, t0:t1],
             )
 
-        def quantize_w1(a):
+        def quantize_w1(a, woven, t0, t1):
             nc.vector.quantize_mx(
-                out=w1_w[a][:].bitcast(FP8X4), scales=w1_sc[a][:], in_=w1_bf[a][:].rearrange("p t m j -> p (t m j)")
+                out=w1_w[a][:, t0 * P : t1 * P].bitcast(FP8X4),
+                scales=w1_sc[a][:, t0 * P : t1 * P],
+                in_=woven[:].rearrange("p t m j -> p (t m j)"),
             )
 
         v_w1 = []
@@ -122,14 +124,14 @@ def tile_list_scrap_join_fit_kernel(
             nc.vector.tensor_copy(picked[:], tab_w[1][:].indirect(offs_sb[:, c * BANK // LANES : (c + 1) * BANK // LANES]))
             v_w1.append(picked)
 
-        weave_w1(0)
-        weave_w1(1)
-        quantize_w1(0)
+        weave_w1(0, w1_bf0, 0, PACK)
+        weave_w1(1, w1_bf0, 0, PACK)
+        quantize_w1(0, w1_bf0, 0, PACK)
         for i in range(2, len(w1_pieces)):
-            weave_w1(i)
+            weave_w1(i, w1_lead, 0, 1)
         for c in range(S // BANK - 1):
             gather_words_1(c, f"v_w1_{c}")
-        quantize_w1(1)
+        quantize_w1(1, w1_lead, 0, 1)
         gather_words_1(S // BANK - 1, "shared")
 
         h = [keep.tile([P, S], F32, name=f"h{t}") for t in range(PACK)]
@@ -159,10 +161,20 @@ def tile_list_scrap_join_fit_kernel(
 
         for t in range(PACK):
             features(t)
+            if t == 0:
+                for i in range(2, len(w1_pieces)):
+                    weave_w1(i, w1_rest, 1, PACK)
+                quantize_w1(1, w1_rest, 1, PACK)
             first = ring.tile([P, PJ], F32)
             nc.vector.tensor_copy(first[:], h[t][:].indirect(pos1_sb[:]))
-            nc.vector.tensor_copy(third[:, t, :], h[t][:].indirect(pos4_sb[:, : PK // 2 // LANES]))
-            nc.vector.tensor_tensor(a1[t][:], h[t][:].indirect(pos2_sb[:]), first[:], ALU.add)
+            if t < PACK - 1:
+                second = ring.tile([P, PJ], F32)
+                nc.vector.tensor_copy(second[:], h[t][:].indirect(pos2_sb[:]))
+                nc.vector.tensor_copy(third[:, t, :], h[t][:].indirect(pos4_sb[:, : PK // 2 // LANES]))
+                nc.gpsimd.tensor_tensor(a1[t][:], first[:], second[:], ALU.add)
+            else:
+                nc.vector.tensor_copy(third[:, t, :], h[t][:].indirect(pos4_sb[:, : PK // 2 // LANES]))
+                nc.vector.tensor_tensor(a1[t][:], h[t][:].indirect(pos2_sb[:]), first[:], ALU.add)
 
         ws_bf = keep.tile([P, N, PACK], BF16, align_bytes=64)
         ws_w = keep.tile([P, N], U32, align_bytes=64)

@@ -47,11 +47,16 @@ def tile_list_scrap_join_fit_kernel(
         pos4_sb = keep.tile([P, PK // LANES], U16)
         tab_sc = keep.tile([P, T], U8, align_bytes=64)
         w4_sc = keep.tile([P, N], U8, align_bytes=64)
-        nc.vector.memset(tab_sc[:].bitcast(I32), 0)
-        nc.vector.memset(w4_sc[:].bitcast(I32), 0)
+        v_sc = [keep.tile([P, S], U8, align_bytes=64, name=f"v_sc{a}") for a in range(PASSES)]
+        nc.gpsimd.memset(tab_sc[32:64, :].bitcast(I32), 0)
+        nc.vector.memset(tab_sc[64:P, :].bitcast(I32), 0)
+        for a in range(PASSES):
+            nc.gpsimd.memset(v_sc[a][:].bitcast(I32), 0)
+        nc.gpsimd.memset(w4_sc[:].bitcast(I32), 0)
+        nc.sync.dma_start(tab_sc[0:32, :].bitcast(I32), tab_scales.rearrange("a q t -> (a q) t").bitcast(I32))
         nc.sync.dma_start(offs_sb[:], offs)
         tab_w = [keep.tile([P, T], U32, align_bytes=64, name=f"tab_w{a}") for a in range(PASSES)]
-        w1_pieces = [(0, 0, 256), (0, 256, 256), (1, 0, 256), (1, 256, 128), (1, 384, 128)]
+        w1_pieces = [(0, 0, 512), (1, 0, 256), (1, 256, 128), (1, 384, 128)]
         w1_raw = [keep.tile([P, PACK, n], F32, name=f"w1_raw{i}") for i, (a, c0, n) in enumerate(w1_pieces)]
 
         def load_words(a):
@@ -62,16 +67,10 @@ def tile_list_scrap_join_fit_kernel(
             rows = w1[a * K_PASS : (a + 1) * K_PASS, :].rearrange("(p j) c -> p j c", j=PACK)
             nc.sync.dma_start(w1_raw[i][:], rows[:, :, c0 : c0 + n])
 
-        load_w1(0)
-        for q in range(4):
-            nc.sync.dma_start(
-                tab_sc[32 * q : 32 * q + 4 * PASSES, :].bitcast(I32),
-                tab_scales[:, 4 * q : 4 * q + 4, :].bitcast(I32),
-            )
         load_words(0)
-        load_w1(1)
+        load_w1(0)
         load_words(1)
-        for i in range(2, len(w1_pieces)):
+        for i in range(1, len(w1_pieces)):
             load_w1(i)
         gain_sb = keep.tile([P, PACK], F32)
         nc.sync.dma_start(gain_sb[:], gain.rearrange("(p t) -> p t", t=PACK))
@@ -92,8 +91,14 @@ def tile_list_scrap_join_fit_kernel(
         preload = keep.tile([P, 1], F32)
         nc.gpsimd.memset(seed[:], 0.0)
         nc.scalar.activation(preload[:], seed[:], ACT.Silu)
-        v_sc = keep.tile([P, S], U8, align_bytes=64)
-        nc.vector.tensor_copy(v_sc[:], tab_sc[:].indirect(offs_sb[:]))
+        picked_sc = keep.tile([P, S], U8, align_bytes=64)
+        nc.vector.tensor_copy(picked_sc[:], tab_sc[:].indirect(offs_sb[:]))
+        for a in range(PASSES):
+            for q in range(4):
+                nc.gpsimd.dma_start(
+                    v_sc[a][32 * q : 32 * q + 4, :].bitcast(I32),
+                    picked_sc[16 * a + 4 * q : 16 * a + 4 * q + 4, :].bitcast(I32),
+                )
         v_w0 = keep.tile([P, S], U32, align_bytes=64)
         nc.vector.tensor_copy(v_w0[:], tab_w[0][:].indirect(offs_sb[:]))
 
@@ -125,14 +130,15 @@ def tile_list_scrap_join_fit_kernel(
             v_w1.append(picked)
 
         weave_w1(0, w1_bf0, 0, PACK)
-        weave_w1(1, w1_bf0, 0, PACK)
         quantize_w1(0, w1_bf0, 0, PACK)
-        for i in range(2, len(w1_pieces)):
+        for i in range(1, len(w1_pieces)):
             weave_w1(i, w1_lead, 0, 1)
+            weave_w1(i, w1_rest, 1, PACK)
         for c in range(S // BANK - 1):
             gather_words_1(c, f"v_w1_{c}")
         quantize_w1(1, w1_lead, 0, 1)
         gather_words_1(S // BANK - 1, "shared")
+        quantize_w1(1, w1_rest, 1, PACK)
 
         h = [keep.tile([P, S], F32, name=f"h{t}") for t in range(PACK)]
         a1 = [keep.tile([P, PJ], F32, name=f"a1_{t}") for t in range(PACK)]
@@ -148,7 +154,7 @@ def tile_list_scrap_join_fit_kernel(
                         lhsT=w1_w[a][:, t * P : (t + 1) * P].bitcast(FP8X4),
                         lhsT_scale=w1_sc[a][:, t * P : (t + 1) * P],
                         rhs=(v_w0[:, cols] if a == 0 else v_w1[c][:]).bitcast(FP8X4),
-                        rhs_scale=v_sc[4 * a : P, cols],
+                        rhs_scale=v_sc[a][:, cols],
                         start=(a == 0),
                         stop=(a == PASSES - 1),
                     )
@@ -161,20 +167,10 @@ def tile_list_scrap_join_fit_kernel(
 
         for t in range(PACK):
             features(t)
-            if t == 0:
-                for i in range(2, len(w1_pieces)):
-                    weave_w1(i, w1_rest, 1, PACK)
-                quantize_w1(1, w1_rest, 1, PACK)
             first = ring.tile([P, PJ], F32)
             nc.vector.tensor_copy(first[:], h[t][:].indirect(pos1_sb[:]))
-            if t < PACK - 1:
-                second = ring.tile([P, PJ], F32)
-                nc.vector.tensor_copy(second[:], h[t][:].indirect(pos2_sb[:]))
-                nc.vector.tensor_copy(third[:, t, :], h[t][:].indirect(pos4_sb[:, : PK // 2 // LANES]))
-                nc.gpsimd.tensor_tensor(a1[t][:], first[:], second[:], ALU.add)
-            else:
-                nc.vector.tensor_copy(third[:, t, :], h[t][:].indirect(pos4_sb[:, : PK // 2 // LANES]))
-                nc.vector.tensor_tensor(a1[t][:], h[t][:].indirect(pos2_sb[:]), first[:], ALU.add)
+            nc.vector.tensor_copy(third[:, t, :], h[t][:].indirect(pos4_sb[:, : PK // 2 // LANES]))
+            nc.vector.tensor_tensor(a1[t][:], h[t][:].indirect(pos2_sb[:]), first[:], ALU.add)
 
         ws_bf = keep.tile([P, N, PACK], BF16, align_bytes=64)
         ws_w = keep.tile([P, N], U32, align_bytes=64)

@@ -20,11 +20,18 @@ ACT = mybir.ActivationFunctionType
 P = 128
 PACK = 4
 K_PASS = P * PACK
-PASSES = K // K_PASS
-BANK = 512
+QUADS = 4
 LANES = 16
+BANK = 512
 J_TILE = 128
-HALF = 3
+CHUNKS = PK // J_TILE
+N_GROUP = 3
+GROUPS = N // (N_GROUP * P)
+WIDTH = N_GROUP * J_TILE
+EARLY = CHUNKS // 2
+
+W1_PIECES = [(0, 0, 512), (1, 0, 256), (1, 256, 128), (1, 384, 128)]
+
 TURN = 2.0 * math.pi
 ROUNDER = 1.5 * 2.0**23
 
@@ -37,8 +44,8 @@ def tile_list_scrap_join_fit_kernel(
         keep = ctx.enter_context(tc.tile_pool(name="keep", bufs=1))
         ring = ctx.enter_context(tc.tile_pool(name="ring", bufs=2))
         deep = ctx.enter_context(tc.tile_pool(name="deep", bufs=4))
-        six = ctx.enter_context(tc.tile_pool(name="six", bufs=6))
-        psum = ctx.enter_context(tc.psum_pool(name="psum", bufs=8))
+        slopes = ctx.enter_context(tc.tile_pool(name="slopes", bufs=6))
+        psum = ctx.enter_context(tc.psum_pool(name="psum", bufs=4))
 
         offs_sb = keep.tile([P, S // LANES], U16)
         pos1_sb = keep.tile([P, PJ // LANES], U16)
@@ -46,56 +53,48 @@ def tile_list_scrap_join_fit_kernel(
         pos3_sb = keep.tile([P, PK // LANES], U16)
         pos4_sb = keep.tile([P, PK // LANES], U16)
         tab_sc = keep.tile([P, T], U8, align_bytes=64)
-        w4_sc = keep.tile([P, N], U8, align_bytes=64)
-        v_sc = [keep.tile([P, S], U8, align_bytes=64, name=f"v_sc{a}") for a in range(PASSES)]
+        v_sc = [keep.tile([P, S], U8, align_bytes=64, name=f"v_sc{a}") for a in range(K // K_PASS)]
         nc.gpsimd.memset(tab_sc[32:64, :].bitcast(I32), 0)
         nc.vector.memset(tab_sc[64:P, :].bitcast(I32), 0)
-        for a in range(PASSES):
-            nc.gpsimd.memset(v_sc[a][:].bitcast(I32), 0)
-        nc.gpsimd.memset(w4_sc[:].bitcast(I32), 0)
+        for plane in v_sc:
+            nc.gpsimd.memset(plane[:].bitcast(I32), 0)
         nc.sync.dma_start(tab_sc[0:32, :].bitcast(I32), tab_scales.rearrange("a q t -> (a q) t").bitcast(I32))
         nc.sync.dma_start(offs_sb[:], offs)
-        tab_w = [keep.tile([P, T], U32, align_bytes=64, name=f"tab_w{a}") for a in range(PASSES)]
-        w1_pieces = [(0, 0, 512), (1, 0, 256), (1, 256, 128), (1, 384, 128)]
-        w1_raw = [keep.tile([P, PACK, n], F32, name=f"w1_raw{i}") for i, (a, c0, n) in enumerate(w1_pieces)]
+        nc.sync.dma_start(pos1_sb[:], pos1)
+        nc.sync.dma_start(pos2_sb[:], pos2)
+        nc.sync.dma_start(pos4_sb[:], pos4)
+        nc.sync.dma_start(pos3_sb[:], pos3)
+
+        tab_w = [keep.tile([P, T], U32, align_bytes=64, name=f"tab_w{a}") for a in range(K // K_PASS)]
+        w1_raw = [
+            keep.tile([P, PACK, n], F32, align_bytes=64, name=f"w1_raw{i}", tag=f"raw{i}")
+            for i, (a, c0, n) in enumerate(W1_PIECES)
+        ]
 
         def load_words(a):
             nc.sync.dma_start(tab_w[a][:].bitcast(I32), tab_words[a].rearrange("p t i -> p (t i)").bitcast(I32))
 
         def load_w1(i):
-            a, c0, n = w1_pieces[i]
+            a, c0, n = W1_PIECES[i]
             rows = w1[a * K_PASS : (a + 1) * K_PASS, :].rearrange("(p j) c -> p j c", j=PACK)
             nc.sync.dma_start(w1_raw[i][:], rows[:, :, c0 : c0 + n])
 
         load_words(0)
         load_w1(0)
         load_words(1)
-        for i in range(1, len(w1_pieces)):
+        for i in range(1, len(W1_PIECES)):
             load_w1(i)
-        gain_sb = keep.tile([P, PACK], F32)
-        nc.sync.dma_start(gain_sb[:], gain.rearrange("(p t) -> p t", t=PACK))
-        nc.sync.dma_start(pos1_sb[:], pos1)
-        nc.sync.dma_start(pos2_sb[:], pos2)
-        nc.sync.dma_start(pos4_sb[:], pos4)
-        nc.sync.dma_start(pos3_sb[:], pos3)
-        ws_raw = keep.tile([P, PACK, N], F32)
-        nc.sync.dma_start(ws_raw[:], ws.rearrange("(p j) n -> p j n", j=PACK))
-        w4_w = keep.tile([P, 2 * N], U8, align_bytes=64)
-        nc.sync.dma_start(w4_w[:].bitcast(I32), w4_words[0].bitcast(I32))
-        for q in range(4):
-            nc.sync.dma_start(
-                w4_sc[32 * q : 32 * q + 4, :].bitcast(I32), w4_scales[0, 4 * q : 4 * q + 4, :].bitcast(I32)
-            )
 
         seed = keep.tile([P, 1], F32)
         preload = keep.tile([P, 1], F32)
         nc.gpsimd.memset(seed[:], 0.0)
         nc.scalar.activation(preload[:], seed[:], ACT.Silu)
-        picked_sc = keep.tile([P, S], U8, align_bytes=64)
+
+        picked_sc = keep.tile([P, S], U8, align_bytes=64, tag="picked")
         nc.vector.tensor_copy(picked_sc[:], tab_sc[:].indirect(offs_sb[:]))
-        for a in range(PASSES):
-            for q in range(4):
-                nc.gpsimd.dma_start(
+        for a, queue in enumerate((nc.scalar, nc.gpsimd)):
+            for q in range(QUADS):
+                queue.dma_start(
                     v_sc[a][32 * q : 32 * q + 4, :].bitcast(I32),
                     picked_sc[16 * a + 4 * q : 16 * a + 4 * q + 4, :].bitcast(I32),
                 )
@@ -103,13 +102,13 @@ def tile_list_scrap_join_fit_kernel(
         nc.vector.tensor_copy(v_w0[:], tab_w[0][:].indirect(offs_sb[:]))
 
         w1_bf0 = keep.tile([P, PACK, P, PACK], BF16, align_bytes=64)
-        w1_lead = keep.tile([P, 1, P, PACK], BF16, align_bytes=64, tag="shared")
+        w1_lead = keep.tile([P, 1, P, PACK], BF16, align_bytes=64, tag="lead")
         w1_rest = keep.tile([P, PACK - 1, P, PACK], BF16, align_bytes=64)
-        w1_w = [keep.tile([P, H], U32, align_bytes=64, name=f"w1_w{a}") for a in range(PASSES)]
-        w1_sc = [keep.tile([P, H], U8, align_bytes=64, name=f"w1_sc{a}") for a in range(PASSES)]
+        w1_w = [keep.tile([P, H], U32, align_bytes=64, name=f"w1_w{a}") for a in range(K // K_PASS)]
+        w1_sc = [keep.tile([P, H], U8, align_bytes=64, name=f"w1_sc{a}") for a in range(K // K_PASS)]
 
         def weave_w1(i, woven, t0, t1):
-            a, c0, n = w1_pieces[i]
+            a, c0, n = W1_PIECES[i]
             nc.scalar.copy(
                 woven[:, :, c0 // PACK : (c0 + n) // PACK, :].rearrange("p t m j -> p m j t"),
                 w1_raw[i][:].rearrange("p j (m t) -> p m j t", t=PACK)[:, :, :, t0:t1],
@@ -124,39 +123,54 @@ def tile_list_scrap_join_fit_kernel(
 
         v_w1 = []
 
-        def gather_words_1(c, tag):
-            picked = keep.tile([P, BANK], U32, align_bytes=64, name=f"v_w1_{c}", tag=tag)
-            nc.vector.tensor_copy(picked[:], tab_w[1][:].indirect(offs_sb[:, c * BANK // LANES : (c + 1) * BANK // LANES]))
-            v_w1.append(picked)
+        def gather_words_1(b, tag):
+            picked_w = keep.tile([P, BANK], U32, align_bytes=64, name=f"v_w1_{b}", tag=tag)
+            columns = offs_sb[:, b * BANK // LANES : (b + 1) * BANK // LANES]
+            nc.vector.tensor_copy(picked_w[:], tab_w[1][:].indirect(columns))
+            v_w1.append(picked_w)
 
         weave_w1(0, w1_bf0, 0, PACK)
         quantize_w1(0, w1_bf0, 0, PACK)
-        for i in range(1, len(w1_pieces)):
+        for i in range(1, len(W1_PIECES)):
             weave_w1(i, w1_lead, 0, 1)
+        for i in range(1, len(W1_PIECES)):
             weave_w1(i, w1_rest, 1, PACK)
-        for c in range(S // BANK - 1):
-            gather_words_1(c, f"v_w1_{c}")
+        for b in range(S // BANK - 1):
+            gather_words_1(b, f"v_w1_{b}")
         quantize_w1(1, w1_lead, 0, 1)
-        gather_words_1(S // BANK - 1, "shared")
+        gather_words_1(S // BANK - 1, "lead")
         quantize_w1(1, w1_rest, 1, PACK)
+
+        gain_sb = keep.tile([P, PACK], F32, align_bytes=64, tag="raw0")
+        nc.sync.dma_start(gain_sb[:], gain.rearrange("(p t) -> p t", t=PACK))
+        ws_raw = keep.tile([P, PACK, N], F32, align_bytes=64, tag="picked")
+        nc.sync.dma_start(ws_raw[:], ws.rearrange("(p j) n -> p j n", j=PACK))
+        w4_w = keep.tile([P, 2 * N], U8, align_bytes=64, tag="raw2")
+        nc.sync.dma_start(w4_w[:].bitcast(I32), w4_words[0].bitcast(I32))
+        w4_sc = keep.tile([P, N], U8, align_bytes=64, tag="raw1")
+        nc.gpsimd.memset(w4_sc[:].bitcast(I32), 0)
+        for q in range(QUADS):
+            nc.sync.dma_start(
+                w4_sc[32 * q : 32 * q + 4, :].bitcast(I32), w4_scales[0, 4 * q : 4 * q + 4, :].bitcast(I32)
+            )
 
         h = [keep.tile([P, S], F32, name=f"h{t}") for t in range(PACK)]
         a1 = [keep.tile([P, PJ], F32, name=f"a1_{t}") for t in range(PACK)]
-        third = keep.tile([P, PACK, PK // 2], F32)
+        early_third = keep.tile([P, PACK, EARLY * J_TILE], F32)
 
-        def features(t):
-            for c in range(S // BANK):
-                cols = slice(c * BANK, (c + 1) * BANK)
+        for t in range(PACK):
+            for b in range(S // BANK):
+                cols = slice(b * BANK, (b + 1) * BANK)
                 acc = psum.tile([P, BANK], F32, name="bank")
-                for a in range(PASSES):
+                for a, words in enumerate((v_w0[:, cols], v_w1[b][:])):
                     nc.tensor.matmul_mx(
                         out=acc[:],
                         lhsT=w1_w[a][:, t * P : (t + 1) * P].bitcast(FP8X4),
                         lhsT_scale=w1_sc[a][:, t * P : (t + 1) * P],
-                        rhs=(v_w0[:, cols] if a == 0 else v_w1[c][:]).bitcast(FP8X4),
+                        rhs=words.bitcast(FP8X4),
                         rhs_scale=v_sc[a][:, cols],
                         start=(a == 0),
-                        stop=(a == PASSES - 1),
+                        stop=(a == K // K_PASS - 1),
                     )
                 edge = deep.tile([P, BANK], F32)
                 nc.scalar.activation(edge[:], acc[:], ACT.Tanh)
@@ -164,39 +178,36 @@ def tile_list_scrap_join_fit_kernel(
                     nc.vector.tensor_scalar(h[t][:, cols], edge[:], gain_sb[:, t : t + 1], None, ALU.mult)
                 else:
                     nc.scalar.activation(h[t][:, cols], edge[:], ACT.Copy, scale=gain_sb[:, t : t + 1])
-
-        for t in range(PACK):
-            features(t)
             first = ring.tile([P, PJ], F32)
             nc.vector.tensor_copy(first[:], h[t][:].indirect(pos1_sb[:]))
-            nc.vector.tensor_copy(third[:, t, :], h[t][:].indirect(pos4_sb[:, : PK // 2 // LANES]))
+            nc.vector.tensor_copy(early_third[:, t, :], h[t][:].indirect(pos4_sb[:, : EARLY * J_TILE // LANES]))
             nc.vector.tensor_tensor(a1[t][:], h[t][:].indirect(pos2_sb[:]), first[:], ALU.add)
 
         ws_bf = keep.tile([P, N, PACK], BF16, align_bytes=64)
         ws_w = keep.tile([P, N], U32, align_bytes=64)
         ws_sc = keep.tile([P, N], U8, align_bytes=64)
-        for u in range(2):
-            cols = slice(u * N // 2, (u + 1) * N // 2)
+        for half in range(2):
+            cols = slice(half * N // 2, (half + 1) * N // 2)
             nc.scalar.copy(
                 ws_bf[:, cols, :].rearrange("p (c i) j -> p c j i", i=4),
                 ws_raw[:, :, cols].rearrange("p j (c i) -> p c j i", i=4),
             )
             nc.vector.quantize_mx(
-                out=ws_w[:, cols].bitcast(FP8X4), scales=ws_sc[:, cols], in_=ws_bf[:, cols, :].rearrange("p n j -> p (n j)")
+                out=ws_w[:, cols].bitcast(FP8X4),
+                scales=ws_sc[:, cols],
+                in_=ws_bf[:, cols, :].rearrange("p n j -> p (n j)"),
             )
 
         out_v = out.rearrange("(b p) j -> p b j", p=P)
-
-        swap = [keep.tile([P, 2 * HALF * J_TILE], F32, name=f"swap{i}") for i in range(2)]
-
-        late = []
+        swap = [keep.tile([P, GROUPS * WIDTH], F32, name=f"swap{i}") for i in range(2)]
+        late_third = []
 
         def third_of(t, c):
-            if c < 2:
-                return third[:, t, c * J_TILE : (c + 1) * J_TILE]
-            return late[t // 2][:, t % 2, (c - 2) * J_TILE : (c - 1) * J_TILE]
+            if c < EARLY:
+                return early_third[:, t, c * J_TILE : (c + 1) * J_TILE]
+            return late_third[t // 2][:, t % 2, (c - EARLY) * J_TILE : (c - EARLY + 1) * J_TILE]
 
-        def products(c):
+        def make_a2(c):
             a2 = swap[c % 2][:, : PACK * J_TILE].rearrange("p (t j) -> p t j", t=PACK)
             for t in range(PACK):
                 nc.vector.tensor_tensor(
@@ -206,30 +217,32 @@ def tile_list_scrap_join_fit_kernel(
                     ALU.mult,
                 )
             a2_bf = keep.tile([P, J_TILE, PACK], BF16, align_bytes=64, name=f"a2_bf{c}", tag=f"late{c}")
-            weave = nc.scalar.copy if c < 2 else nc.vector.tensor_copy
-            weave(
-                a2_bf[:].rearrange("p (c i) t -> p c t i", i=4), a2.rearrange("p t (c i) -> p c t i", i=4)
-            )
+            weave = nc.scalar.copy if c < EARLY else nc.vector.tensor_copy
+            weave(a2_bf[:].rearrange("p (c i) t -> p c t i", i=4), a2.rearrange("p t (c i) -> p c t i", i=4))
             a2_w = ring.tile([P, J_TILE], U32, align_bytes=64)
             a2_sc = ring.tile([P, J_TILE], U8, align_bytes=64)
             nc.vector.quantize_mx(
                 out=a2_w[:].bitcast(FP8X4), scales=a2_sc[:], in_=a2_bf[:].rearrange("p j t -> p (j t)")
             )
-            if c < 2:
-                pair = keep.tile([P, 2, PK // 2], F32, align_bytes=64, name=f"late_third{c}", tag=f"late{c}")
+            if c < EARLY:
+                pair = keep.tile(
+                    [P, 2, PK - EARLY * J_TILE], F32, align_bytes=64, name=f"late_third{c}", tag=f"late{c}"
+                )
                 for i in range(2):
-                    nc.vector.tensor_copy(pair[:, i, :], h[2 * c + i][:].indirect(pos4_sb[:, PK // 2 // LANES :]))
-                late.append(pair)
+                    nc.vector.tensor_copy(
+                        pair[:, i, :], h[2 * c + i][:].indirect(pos4_sb[:, EARLY * J_TILE // LANES :])
+                    )
+                late_third.append(pair)
             return a2_w, a2_sc
 
         def multiply(c, a2_w, a2_sc):
             parts = []
             leans = []
-            for u in range(2):
+            for g in range(GROUPS):
                 phase = psum.tile([P, BANK], F32, name="bank")
-                lean = psum.tile([P, BANK], F32, name="bank")
-                for b in range(HALF):
-                    n0 = (u * HALF + b) * P
+                lean = psum.tile([P, BANK], F32, name="lean")
+                for b in range(N_GROUP):
+                    n0 = (g * N_GROUP + b) * P
                     nc.tensor.matmul_mx(
                         out=phase[:, b * J_TILE : (b + 1) * J_TILE],
                         lhsT=ws_w[:, n0 : n0 + P].bitcast(FP8X4),
@@ -239,8 +252,8 @@ def tile_list_scrap_join_fit_kernel(
                         start=True,
                         stop=True,
                     )
-                for b in range(HALF):
-                    n0 = (u * HALF + b) * P
+                for b in range(N_GROUP):
+                    n0 = (g * N_GROUP + b) * P
                     nc.tensor.matmul_mx(
                         out=lean[:, b * J_TILE : (b + 1) * J_TILE],
                         lhsT=w4_w[:, 2 * n0 : 2 * (n0 + P)].bitcast(FP4X4),
@@ -250,51 +263,51 @@ def tile_list_scrap_join_fit_kernel(
                         start=True,
                         stop=True,
                     )
-                width = HALF * J_TILE
-                turns = swap[c % 2][:, u * width : (u + 1) * width]
-                whole = deep.tile([P, width], U32)
-                slope = six.tile([P, width], F32)
-                nc.scalar.activation(turns, phase[:, :width], ACT.Copy, scale=1.0 / TURN)
-                if c == PK // J_TILE - 1:
+                turns = swap[c % 2][:, g * WIDTH : (g + 1) * WIDTH]
+                whole = deep.tile([P, WIDTH], U32)
+                slope = slopes.tile([P, WIDTH], F32)
+                nc.scalar.activation(turns, phase[:, :WIDTH], ACT.Copy, scale=1.0 / TURN)
+                if c == CHUNKS - 1:
                     nc.vector.tensor_scalar(
-                        whole[:].bitcast(I32), phase[:, :width], 1.0 / TURN, ROUNDER, ALU.mult, ALU.add
+                        whole[:].bitcast(I32), phase[:, :WIDTH], 1.0 / TURN, ROUNDER, ALU.mult, ALU.add
                     )
                 else:
-                    nc.scalar.activation(whole[:], phase[:, :width], ACT.Copy, scale=1.0 / TURN, bias=ROUNDER)
+                    nc.scalar.activation(whole[:], phase[:, :WIDTH], ACT.Copy, scale=1.0 / TURN, bias=ROUNDER)
                 parts.append((turns, whole, slope))
                 leans.append(lean)
-            for u in range(2):
-                nc.scalar.activation(parts[u][2][:], leans[u][:, : HALF * J_TILE], ACT.Tanh)
+            for (turns, whole, slope), lean in zip(parts, leans):
+                nc.scalar.activation(slope[:], lean[:, :WIDTH], ACT.Tanh)
             return parts
 
-        def reduce_phase(parts):
+        def sine(parts):
             waves = []
             for turns, whole, slope in parts:
-                rest = ring.tile([P, HALF * J_TILE], F32)
+                rest = ring.tile([P, WIDTH], F32)
                 nc.vector.scalar_tensor_tensor(
                     rest[:], whole[:].bitcast(I32), ROUNDER, turns, ALU.subtract, ALU.subtract
                 )
-                wave = deep.tile([P, HALF * J_TILE], F32)
+                wave = deep.tile([P, WIDTH], F32)
                 nc.scalar.activation(wave[:], rest[:], ACT.Sin, scale=-TURN)
                 waves.append((wave, slope))
             return waves
 
         def finish(c, waves):
-            for u, (wave, slope) in enumerate(waves):
-                fit = deep.tile([P, HALF, J_TILE], F32)
+            for g, (wave, slope) in enumerate(waves):
+                fit = deep.tile([P, N_GROUP, J_TILE], F32)
                 nc.vector.tensor_tensor(fit[:].rearrange("p b j -> p (b j)"), wave[:], slope[:], ALU.mult)
-                nc.sync.dma_start(out_v[:, u * HALF : (u + 1) * HALF, c * J_TILE : (c + 1) * J_TILE], fit[:])
+                nc.sync.dma_start(
+                    out_v[:, g * N_GROUP : (g + 1) * N_GROUP, c * J_TILE : (c + 1) * J_TILE], fit[:]
+                )
 
-        chunks = PK // J_TILE
+        codes = {c: make_a2(c) for c in range(EARLY)}
         parts = {}
         waves = {}
-        codes = {0: products(0), 1: products(1)}
-        for step in range(chunks + 2):
-            if 2 <= step < chunks:
-                codes[step] = products(step)
-            if step < chunks:
+        for step in range(CHUNKS + 2):
+            if EARLY <= step < CHUNKS:
+                codes[step] = make_a2(step)
+            if step < CHUNKS:
                 parts[step] = multiply(step, *codes[step])
-            if 2 <= step:
+            if step >= 2:
                 finish(step - 2, waves[step - 2])
-            if 1 <= step <= chunks:
-                waves[step - 1] = reduce_phase(parts[step - 1])
+            if 1 <= step <= CHUNKS:
+                waves[step - 1] = sine(parts[step - 1])

import math
from contextlib import ExitStack

import concourse.mybir as mybir

T, S, PJ, PK, K, H, N = 4096, 2048, 1024, 512, 1024, 512, 768
FLOPS = 2 * K * H * S + 2 * 2 * H * N * PK

F32 = mybir.dt.float32
BF16 = mybir.dt.bfloat16
I32 = mybir.dt.int32
U32 = mybir.dt.uint32
U16 = mybir.dt.uint16
U8 = mybir.dt.uint8
FP8X4 = mybir.dt.float8_e4m3fn_x4
FP4X4 = mybir.dt.float4_e2m1fn_x4
ALU = mybir.AluOpType
ACT = mybir.ActivationFunctionType

P = 128
PACK = 4
K_PASS = P * PACK
QUADS = 4
LANES = 16
BANK = 512
J_TILE = 128
CHUNKS = PK // J_TILE
N_GROUP = 3
GROUPS = N // (N_GROUP * P)
WIDTH = N_GROUP * J_TILE
EARLY = CHUNKS // 2

W1_PIECES = [(0, 0, 512), (1, 0, 256), (1, 256, 128), (1, 384, 128)]

TURN = 2.0 * math.pi
ROUNDER = 1.5 * 2.0**23


def tile_list_scrap_join_fit_kernel(
    tc, tab_words, tab_scales, offs, pos1, pos2, pos3, pos4, w1, gain, ws, w4_words, w4_scales, out
):
    nc = tc.nc
    with ExitStack() as ctx:
        keep = ctx.enter_context(tc.tile_pool(name="keep", bufs=1))
        ring = ctx.enter_context(tc.tile_pool(name="ring", bufs=2))
        deep = ctx.enter_context(tc.tile_pool(name="deep", bufs=4))
        slopes = ctx.enter_context(tc.tile_pool(name="slopes", bufs=6))
        psum = ctx.enter_context(tc.psum_pool(name="psum", bufs=4))

        offs_sb = keep.tile([P, S // LANES], U16)
        pos1_sb = keep.tile([P, PJ // LANES], U16)
        pos2_sb = keep.tile([P, PJ // LANES], U16)
        pos3_sb = keep.tile([P, PK // LANES], U16)
        pos4_sb = keep.tile([P, PK // LANES], U16)
        tab_sc = keep.tile([P, T], U8, align_bytes=64)
        v_sc = [keep.tile([P, S], U8, align_bytes=64, name=f"v_sc{a}") for a in range(K // K_PASS)]
        nc.gpsimd.memset(tab_sc[32:64, :].bitcast(I32), 0)
        nc.vector.memset(tab_sc[64:P, :].bitcast(I32), 0)
        for plane in v_sc:
            nc.gpsimd.memset(plane[:].bitcast(I32), 0)
        nc.sync.dma_start(tab_sc[0:32, :].bitcast(I32), tab_scales.rearrange("a q t -> (a q) t").bitcast(I32))
        nc.sync.dma_start(offs_sb[:], offs)
        nc.sync.dma_start(pos1_sb[:], pos1)
        nc.sync.dma_start(pos2_sb[:], pos2)
        nc.sync.dma_start(pos4_sb[:], pos4)
        nc.sync.dma_start(pos3_sb[:], pos3)

        tab_w = [keep.tile([P, T], U32, align_bytes=64, name=f"tab_w{a}") for a in range(K // K_PASS)]
        w1_raw = [
            keep.tile([P, PACK, n], F32, align_bytes=64, name=f"w1_raw{i}", tag=f"raw{i}")
            for i, (a, c0, n) in enumerate(W1_PIECES)
        ]

        def load_words(a):
            nc.sync.dma_start(tab_w[a][:].bitcast(I32), tab_words[a].rearrange("p t i -> p (t i)").bitcast(I32))

        def load_w1(i):
            a, c0, n = W1_PIECES[i]
            rows = w1[a * K_PASS : (a + 1) * K_PASS, :].rearrange("(p j) c -> p j c", j=PACK)
            nc.sync.dma_start(w1_raw[i][:], rows[:, :, c0 : c0 + n])

        load_words(0)
        load_w1(0)
        load_words(1)
        for i in range(1, len(W1_PIECES)):
            load_w1(i)

        seed = keep.tile([P, 1], F32)
        preload = keep.tile([P, 1], F32)
        nc.gpsimd.memset(seed[:], 0.0)
        nc.scalar.activation(preload[:], seed[:], ACT.Silu)

        picked_sc = keep.tile([P, S], U8, align_bytes=64, tag="picked")
        nc.vector.tensor_copy(picked_sc[:], tab_sc[:].indirect(offs_sb[:]))
        for a, queue in enumerate((nc.scalar, nc.gpsimd)):
            for q in range(QUADS):
                queue.dma_start(
                    v_sc[a][32 * q : 32 * q + 4, :].bitcast(I32),
                    picked_sc[16 * a + 4 * q : 16 * a + 4 * q + 4, :].bitcast(I32),
                )
        v_w0 = keep.tile([P, S], U32, align_bytes=64)
        nc.vector.tensor_copy(v_w0[:], tab_w[0][:].indirect(offs_sb[:]))

        w1_bf0 = keep.tile([P, PACK, P, PACK], BF16, align_bytes=64)
        w1_lead = keep.tile([P, 1, P, PACK], BF16, align_bytes=64, tag="lead")
        w1_rest = keep.tile([P, PACK - 1, P, PACK], BF16, align_bytes=64)
        w1_w = [keep.tile([P, H], U32, align_bytes=64, name=f"w1_w{a}") for a in range(K // K_PASS)]
        w1_sc = [keep.tile([P, H], U8, align_bytes=64, name=f"w1_sc{a}") for a in range(K // K_PASS)]

        def weave_w1(i, woven, t0, t1):
            a, c0, n = W1_PIECES[i]
            nc.scalar.copy(
                woven[:, :, c0 // PACK : (c0 + n) // PACK, :].rearrange("p t m j -> p m j t"),
                w1_raw[i][:].rearrange("p j (m t) -> p m j t", t=PACK)[:, :, :, t0:t1],
            )

        def quantize_w1(a, woven, t0, t1):
            nc.vector.quantize_mx(
                out=w1_w[a][:, t0 * P : t1 * P].bitcast(FP8X4),
                scales=w1_sc[a][:, t0 * P : t1 * P],
                in_=woven[:].rearrange("p t m j -> p (t m j)"),
            )

        v_w1 = []

        def gather_words_1(b, tag):
            picked_w = keep.tile([P, BANK], U32, align_bytes=64, name=f"v_w1_{b}", tag=tag)
            columns = offs_sb[:, b * BANK // LANES : (b + 1) * BANK // LANES]
            nc.vector.tensor_copy(picked_w[:], tab_w[1][:].indirect(columns))
            v_w1.append(picked_w)

        weave_w1(0, w1_bf0, 0, PACK)
        quantize_w1(0, w1_bf0, 0, PACK)
        for i in range(1, len(W1_PIECES)):
            weave_w1(i, w1_lead, 0, 1)
        for i in range(1, len(W1_PIECES)):
            weave_w1(i, w1_rest, 1, PACK)
        for b in range(S // BANK - 1):
            gather_words_1(b, f"v_w1_{b}")
        quantize_w1(1, w1_lead, 0, 1)
        gather_words_1(S // BANK - 1, "lead")
        quantize_w1(1, w1_rest, 1, PACK)

        gain_sb = keep.tile([P, PACK], F32, align_bytes=64, tag="raw0")
        nc.sync.dma_start(gain_sb[:], gain.rearrange("(p t) -> p t", t=PACK))
        ws_raw = keep.tile([P, PACK, N], F32, align_bytes=64, tag="picked")
        nc.sync.dma_start(ws_raw[:], ws.rearrange("(p j) n -> p j n", j=PACK))
        w4_w = keep.tile([P, 2 * N], U8, align_bytes=64, tag="raw2")
        nc.sync.dma_start(w4_w[:].bitcast(I32), w4_words[0].bitcast(I32))
        w4_sc = keep.tile([P, N], U8, align_bytes=64, tag="raw1")
        nc.gpsimd.memset(w4_sc[:].bitcast(I32), 0)
        for q in range(QUADS):
            nc.sync.dma_start(
                w4_sc[32 * q : 32 * q + 4, :].bitcast(I32), w4_scales[0, 4 * q : 4 * q + 4, :].bitcast(I32)
            )

        h = [keep.tile([P, S], F32, name=f"h{t}") for t in range(PACK)]
        a1 = [keep.tile([P, PJ], F32, name=f"a1_{t}") for t in range(PACK)]
        early_third = keep.tile([P, PACK, EARLY * J_TILE], F32)

        for t in range(PACK):
            for b in range(S // BANK):
                cols = slice(b * BANK, (b + 1) * BANK)
                acc = psum.tile([P, BANK], F32, name="bank")
                for a, words in enumerate((v_w0[:, cols], v_w1[b][:])):
                    nc.tensor.matmul_mx(
                        out=acc[:],
                        lhsT=w1_w[a][:, t * P : (t + 1) * P].bitcast(FP8X4),
                        lhsT_scale=w1_sc[a][:, t * P : (t + 1) * P],
                        rhs=words.bitcast(FP8X4),
                        rhs_scale=v_sc[a][:, cols],
                        start=(a == 0),
                        stop=(a == K // K_PASS - 1),
                    )
                edge = deep.tile([P, BANK], F32)
                nc.scalar.activation(edge[:], acc[:], ACT.Tanh)
                if t == 0:
                    nc.vector.tensor_scalar(h[t][:, cols], edge[:], gain_sb[:, t : t + 1], None, ALU.mult)
                else:
                    nc.scalar.activation(h[t][:, cols], edge[:], ACT.Copy, scale=gain_sb[:, t : t + 1])
            first = ring.tile([P, PJ], F32)
            nc.vector.tensor_copy(first[:], h[t][:].indirect(pos1_sb[:]))
            nc.vector.tensor_copy(early_third[:, t, :], h[t][:].indirect(pos4_sb[:, : EARLY * J_TILE // LANES]))
            nc.vector.tensor_tensor(a1[t][:], h[t][:].indirect(pos2_sb[:]), first[:], ALU.add)

        ws_bf = keep.tile([P, N, PACK], BF16, align_bytes=64)
        ws_w = keep.tile([P, N], U32, align_bytes=64)
        ws_sc = keep.tile([P, N], U8, align_bytes=64)
        for half in range(2):
            cols = slice(half * N // 2, (half + 1) * N // 2)
            nc.scalar.copy(
                ws_bf[:, cols, :].rearrange("p (c i) j -> p c j i", i=4),
                ws_raw[:, :, cols].rearrange("p j (c i) -> p c j i", i=4),
            )
            nc.vector.quantize_mx(
                out=ws_w[:, cols].bitcast(FP8X4),
                scales=ws_sc[:, cols],
                in_=ws_bf[:, cols, :].rearrange("p n j -> p (n j)"),
            )

        out_v = out.rearrange("(b p) j -> p b j", p=P)
        swap = [keep.tile([P, GROUPS * WIDTH], F32, name=f"swap{i}") for i in range(2)]
        late_third = []

        def third_of(t, c):
            if c < EARLY:
                return early_third[:, t, c * J_TILE : (c + 1) * J_TILE]
            return late_third[t // 2][:, t % 2, (c - EARLY) * J_TILE : (c - EARLY + 1) * J_TILE]

        def make_a2(c):
            a2 = swap[c % 2][:, : PACK * J_TILE].rearrange("p (t j) -> p t j", t=PACK)
            for t in range(PACK):
                nc.vector.tensor_tensor(
                    a2[:, t, :],
                    a1[t][:].indirect(pos3_sb[:, c * J_TILE // LANES : (c + 1) * J_TILE // LANES]),
                    third_of(t, c),
                    ALU.mult,
                )
            a2_bf = keep.tile([P, J_TILE, PACK], BF16, align_bytes=64, name=f"a2_bf{c}", tag=f"late{c}")
            weave = nc.scalar.copy if c < EARLY else nc.vector.tensor_copy
            weave(a2_bf[:].rearrange("p (c i) t -> p c t i", i=4), a2.rearrange("p t (c i) -> p c t i", i=4))
            a2_w = ring.tile([P, J_TILE], U32, align_bytes=64)
            a2_sc = ring.tile([P, J_TILE], U8, align_bytes=64)
            nc.vector.quantize_mx(
                out=a2_w[:].bitcast(FP8X4), scales=a2_sc[:], in_=a2_bf[:].rearrange("p j t -> p (j t)")
            )
            if c < EARLY:
                pair = keep.tile(
                    [P, 2, PK - EARLY * J_TILE], F32, align_bytes=64, name=f"late_third{c}", tag=f"late{c}"
                )
                for i in range(2):
                    nc.vector.tensor_copy(
                        pair[:, i, :], h[2 * c + i][:].indirect(pos4_sb[:, EARLY * J_TILE // LANES :])
                    )
                late_third.append(pair)
            return a2_w, a2_sc

        def multiply(c, a2_w, a2_sc):
            parts = []
            leans = []
            for g in range(GROUPS):
                phase = psum.tile([P, BANK], F32, name="bank")
                lean = psum.tile([P, BANK], F32, name="lean")
                for b in range(N_GROUP):
                    n0 = (g * N_GROUP + b) * P
                    nc.tensor.matmul_mx(
                        out=phase[:, b * J_TILE : (b + 1) * J_TILE],
                        lhsT=ws_w[:, n0 : n0 + P].bitcast(FP8X4),
                        lhsT_scale=ws_sc[:, n0 : n0 + P],
                        rhs=a2_w[:].bitcast(FP8X4),
                        rhs_scale=a2_sc[:],
                        start=True,
                        stop=True,
                    )
                for b in range(N_GROUP):
                    n0 = (g * N_GROUP + b) * P
                    nc.tensor.matmul_mx(
                        out=lean[:, b * J_TILE : (b + 1) * J_TILE],
                        lhsT=w4_w[:, 2 * n0 : 2 * (n0 + P)].bitcast(FP4X4),
                        lhsT_scale=w4_sc[:, n0 : n0 + P],
                        rhs=a2_w[:].bitcast(FP8X4),
                        rhs_scale=a2_sc[:],
                        start=True,
                        stop=True,
                    )
                turns = swap[c % 2][:, g * WIDTH : (g + 1) * WIDTH]
                whole = deep.tile([P, WIDTH], U32)
                slope = slopes.tile([P, WIDTH], F32)
                nc.scalar.activation(turns, phase[:, :WIDTH], ACT.Copy, scale=1.0 / TURN)
                if c == CHUNKS - 1:
                    nc.vector.tensor_scalar(
                        whole[:].bitcast(I32), phase[:, :WIDTH], 1.0 / TURN, ROUNDER, ALU.mult, ALU.add
                    )
                else:
                    nc.scalar.activation(whole[:], phase[:, :WIDTH], ACT.Copy, scale=1.0 / TURN, bias=ROUNDER)
                parts.append((turns, whole, slope))
                leans.append(lean)
            for (turns, whole, slope), lean in zip(parts, leans):
                nc.scalar.activation(slope[:], lean[:, :WIDTH], ACT.Tanh)
            return parts

        def sine(parts):
            waves = []
            for turns, whole, slope in parts:
                rest = ring.tile([P, WIDTH], F32)
                nc.vector.scalar_tensor_tensor(
                    rest[:], whole[:].bitcast(I32), ROUNDER, turns, ALU.subtract, ALU.subtract
                )
                wave = deep.tile([P, WIDTH], F32)
                nc.scalar.activation(wave[:], rest[:], ACT.Sin, scale=-TURN)
                waves.append((wave, slope))
            return waves

        def finish(c, waves):
            for g, (wave, slope) in enumerate(waves):
                fit = deep.tile([P, N_GROUP, J_TILE], F32)
                nc.vector.tensor_tensor(fit[:].rearrange("p b j -> p (b j)"), wave[:], slope[:], ALU.mult)
                nc.sync.dma_start(
                    out_v[:, g * N_GROUP : (g + 1) * N_GROUP, c * J_TILE : (c + 1) * J_TILE], fit[:]
                )

        codes = {c: make_a2(c) for c in range(EARLY)}
        parts = {}
        waves = {}
        for step in range(CHUNKS + 2):
            if EARLY <= step < CHUNKS:
                codes[step] = make_a2(step)
            if step < CHUNKS:
                parts[step] = multiply(step, *codes[step])
            if step >= 2:
                finish(step - 2, waves[step - 2])
            if 1 <= step <= CHUNKS:
                waves[step - 1] = sine(parts[step - 1])
